import numpy as np
import ml_dtypes


def mxq(x, axis, fmt="e4m3"):
    dtype, down = {"e4m3": (ml_dtypes.float8_e4m3fn, 7), "e5m2": (ml_dtypes.float8_e5m2, 14)}[fmt]
    v = np.moveaxis(np.asarray(x, np.float32).astype(ml_dtypes.bfloat16).astype(np.float64), axis, -1)
    blocks = v.reshape(v.shape[:-1] + (-1, 32))
    amax = np.abs(blocks).max(-1, keepdims=True)
    byte = np.maximum(np.where(amax > 0, np.frexp(amax)[1] - 1 + 127, 0) - down, 1)
    scale = np.exp2(byte - 127.0)
    codes = (blocks / scale).astype(np.float32).astype(dtype).astype(np.float64)
    return np.moveaxis((codes * scale).reshape(v.shape), -1, axis)


WIDE = False


def mx_kscale(k):
    if not WIDE:
        return np.ones(k)
    levels = np.array([10, -10, 5, -5, 0])
    if k % 512:
        return np.exp2(np.random.permutation(np.resize(levels, k // 32))).repeat(32)
    a = np.empty((k // 512, 16))
    for p in range(k // 512):
        a[p, :8] = np.random.permutation(np.resize(levels, 8))
        for g in range(8):
            far = levels[np.abs(levels - a[p, g]) >= 10]
            a[p, g + 8] = far[np.random.randint(len(far))]
    return np.exp2(a.ravel()).repeat(32)


def f64(x):
    return np.asarray(x).astype(np.float64)


def striped(idx):
    return np.tile(idx.reshape(-1, 16).T, (8, 1)).astype(np.uint16)


def unstriped(offs):
    return offs[:16].T.reshape(-1).astype(np.int64)


def striped8(idx):
    return np.concatenate([x.reshape(-1, 16).T for x in idx]).astype(np.uint16)


def runs(offs, k):
    lists = np.stack([offs[16 * r : 16 * r + 16].T.reshape(-1) for r in range(8)]).astype(np.int64)
    return lists[np.arange(k) % 512 // 64]


def pack_weight(w):
    k, n = w.shape
    w = f64(np.asarray(w, np.float32).astype(ml_dtypes.bfloat16)).reshape(k // 32, 32, n)
    amax = np.abs(w).max(1)
    byte = np.clip(np.where(amax > 0, np.frexp(amax)[1] - 1 + 127 - 7, 1), 1, 254)
    scaled = (w * np.exp2(127.0 - byte)[:, None, :]).reshape(k, n).astype(np.float32)
    words = np.ascontiguousarray(scaled.reshape(k // 512, 128, 4, n).transpose(0, 1, 3, 2)).astype(ml_dtypes.float8_e4m3fn).view(np.uint8)
    return words, np.ascontiguousarray(byte.astype(np.uint8).reshape(k // 512, 16, n))


def unpack_weight(words, scales):
    g, p, n, _ = words.shape
    vals = np.ascontiguousarray(words).view(ml_dtypes.float8_e4m3fn).astype(np.float64) * np.repeat(np.exp2(scales.astype(np.float64) - 127.0), 8, axis=1)[..., None]
    return vals.transpose(0, 1, 3, 2).reshape(g * 512, n)

def planes(y):
    n, m = y.shape
    v = y.astype(np.float32).astype(ml_dtypes.bfloat16).astype(np.float64).reshape(n // 32, 32, m)
    top = np.abs(v).max(1)
    byte = np.clip(np.where(top > 0, np.frexp(top)[1] - 1 + 127 - 7, 1), 1, 254)
    codes = (v * np.exp2(127.0 - byte)[:, None, :]).reshape(n, m).astype(np.float32).astype(ml_dtypes.float8_e4m3fn).view(np.uint8)
    words = codes.reshape(n // 512, 128, 4, m).transpose(0, 1, 3, 2)
    return np.ascontiguousarray(words), np.ascontiguousarray(byte.astype(np.uint8).reshape(n // 512, 16, m))


K, T, S, H, C = 512, 2048, 512, 512, 512


def setup_inputs():
    n = np.random.standard_normal
    s = mx_kscale(K)[:, None]
    packed_xT = pack_weight(n((K, T)) * s)
    packed_w1 = pack_weight(n((K, H)) / np.sqrt(K) / s)
    return {
        "x_words": packed_xT[0],
        "x_scales": packed_xT[1],
        "w1_words": packed_w1[0],
        "w1_scales": packed_w1[1],
        "gs": (np.random.uniform(0.5, 1.5, (K, 1)) / s).astype(np.float32),
        "offs": striped(np.random.permutation(T)[:S]),
        "n1": striped8(np.stack([np.random.permutation(S) for _ in range(8)])),
        "n2": striped8(np.stack([np.random.permutation(S) for _ in range(8)])),
        "n3": striped8(np.stack([np.random.permutation(S) for _ in range(8)])),
        "cand": striped(np.random.permutation(T)[:C]),
        "n4": striped8(np.stack([np.random.permutation(S) for _ in range(8)])),
        "n5": striped8(np.stack([np.random.permutation(S) for _ in range(8)])),
    }


def reference(x_words, x_scales, w1_words, w1_scales, gs, offs, n1, n2, n3, cand, n4, n5):
    x_cand = unpack_weight(x_words, x_scales)[:, unstriped(cand)]
    xq = unpack_weight(x_words, x_scales)[:, unstriped(offs)]
    y = unpack_weight(w1_words, w1_scales).T @ xq
    ex = np.exp(0.5 * y)
    z = f64(gs) * (np.log((ex + ex[np.arange(H)[:, None], runs(n1, H)]) / (ex[np.arange(H)[:, None], runs(n2, H)] + ex[np.arange(H)[:, None], runs(n3, H)])))
    s = 0.0625 * ((x_cand.T @ mxq(z, 0, "e4m3")))
    st = s - (s[np.arange(C)[:, None], runs(n4, C)])
    out_0 = np.maximum(st, st[np.arange(C)[:, None], runs(n5, C)])
    return (out_0,) + planes(out_0)

@@ -1,0 +1,195 @@
+from contextlib import ExitStack
+
+import concourse.mybir as mybir
+
+FLOPS = 2 * 512 * 512 * 512 * 2
+
+F32 = mybir.dt.float32
+BF16 = mybir.dt.bfloat16
+I32 = mybir.dt.int32
+U32 = mybir.dt.uint32
+U16 = mybir.dt.uint16
+U8 = mybir.dt.uint8
+FP8X4 = mybir.dt.float8_e4m3fn_x4
+ACT = mybir.ActivationFunctionType
+ALU = mybir.AluOpType
+
+P = 128
+PACK = 4
+T = 2048
+S = 512
+WIN = 1024
+Z_CHUNKS = ((0, 128), (128, 256), (256, 384), (384, 512))
+EARLY = 384
+OUT_CHUNKS = ((0, 256), (256, 384), (384, 512))
+
+
+def tile_picked_candoddshopmx_none_po_kernel(tc, x_words, x_scales, w1_words, w1_scales, gs, offs, n1, n2, n3, cand, n4, n5, out_0, out_1, out_2):
+    nc = tc.nc
+    with ExitStack() as ctx:
+        held = ctx.enter_context(tc.tile_pool(name="held", bufs=1))
+        psum = ctx.enter_context(tc.psum_pool(name="psum", bufs=1))
+
+        def sb(name, shape, dtype):
+            return held.tile(shape, dtype, name=name, align_bytes=64)
+
+        def load_list(name, src):
+            tile = sb(name, [P, S // 16], U16)
+            nc.sync.dma_start(tile[:], src)
+            return tile
+
+        def load_scales(name, src, width, queues):
+            tile = sb(name, [P, width], U8)
+            nc.vector.memset(tile[:].bitcast(I32), 0)
+            for q in range(4):
+                queues[q].dma_start(tile[32 * q : 32 * q + 4, :].bitcast(I32), src[0, 4 * q : 4 * q + 4, :].bitcast(I32))
+            return tile
+
+        def load_words(name, src, width, queue):
+            tile = sb(name, [P, width], I32)
+            queue.dma_start(tile[:], src[0].rearrange("p n r -> p (n r)").bitcast(I32))
+            return tile
+
+        def deal(name, src, dtype):
+            tile = sb(name, [P, S], dtype)
+            nc.vector.tensor_copy(tile[:].rearrange("p (t m) -> p m t", t=PACK), src[:].rearrange("p (m t) -> p m t", t=PACK))
+            return tile
+
+        def window(name):
+            tile = sb(name, [P, WIN], F32)
+            nc.vector.memset(tile[:, S:], 0.0)
+            return tile
+
+        def product(out, words, scales, t, rhs_words, rhs_scales):
+            nc.tensor.matmul_mx(
+                out,
+                lhsT=words[:, P * t : P * (t + 1)].bitcast(FP8X4),
+                lhsT_scale=scales[:, P * t : P * (t + 1)],
+                rhs=rhs_words.bitcast(FP8X4),
+                rhs_scale=rhs_scales,
+                start=True,
+                stop=True,
+            )
+
+        def interleaved(ap):
+            return ap.rearrange("p (c i t) -> p c t i", i=4, t=PACK)
+
+        def planar(ap):
+            return ap.rearrange("p t (c i) -> p c t i", i=4)
+
+        offs_l = load_list("offs_l", offs)
+        ww = load_words("ww", w1_words, S, nc.scalar)
+        xs = load_scales("xs", x_scales, T, (nc.sync, nc.sync, nc.scalar, nc.scalar))
+        xw = load_words("xw", x_words, T, nc.sync)
+        ws = load_scales("ws", w1_scales, S, (nc.scalar,) * 4)
+        cand_l = load_list("cand_l", cand)
+        n1_l = load_list("n1_l", n1)
+        n2_l = load_list("n2_l", n2)
+        n3_l = load_list("n3_l", n3)
+        gain = sb("gain", [P, PACK], F32)
+        nc.sync.dma_start(gain[:], gs.rearrange("(p t) o -> p (t o)", t=PACK))
+        n4_l = load_list("n4_l", n4)
+        n5_l = load_list("n5_l", n5)
+
+        ex_win = [window("ex_win%d" % t) for t in range(PACK)]
+        y_win = [sb("y_win%d" % t, [P, S], F32) for t in range(PACK)]
+        banks = [psum.tile([P, S], F32, name="bank%d" % b) for b in range(8)]
+
+        wwd = deal("wwd", ww, I32)
+        qw = sb("qw", [P, S], I32)
+        qs = sb("qs", [P, S], U8)
+        cw = sb("cw", [P, S], I32)
+        cs = sb("cs", [P, S], U8)
+        nc.vector.tensor_copy(qw[:].bitcast(U32), xw[:].bitcast(U32).indirect(offs_l[:]))
+        nc.vector.tensor_copy(qs[:], xs[:].indirect(offs_l[:]))
+        wsd = deal("wsd", ws, U8)
+        for t in range(PACK):
+            product(banks[t][:], wwd, wsd, t, qw[:], qs[:])
+        nc.vector.tensor_copy(cw[:].bitcast(U32), xw[:].bitcast(U32).indirect(cand_l[:]))
+
+        ex_plain = sb("ex_plain", [P, PACK, S], F32)
+        second = sb("second", [P, PACK, S], F32)
+        num = sb("num", [P, PACK, S], F32)
+        den = sb("den", [P, PACK, S], F32)
+
+        def exp_out(t):
+            nc.scalar.activation(ex_win[t][:, :S], banks[t][:], ACT.Exp, scale=0.5)
+            if t == 0:
+                nc.vector.tensor_scalar(y_win[t][:, :S], banks[t][:], 0.5, None, ALU.mult)
+                nc.vector.tensor_copy(ex_plain[:, t, :], ex_win[t][:, :S])
+            else:
+                nc.sync.dma_start(ex_plain[:, t, :], ex_win[t][:, :S])
+
+        def sums(t, a, b):
+            nc.vector.tensor_tensor(num[:, t, a:b], ex_win[t][:].indirect(n1_l[:, a // 16 : b // 16]), ex_plain[:, t, a:b], ALU.add)
+            nc.vector.tensor_tensor(den[:, t, a:b], ex_win[t][:].indirect(n3_l[:, a // 16 : b // 16]), second[:, t, a:b], ALU.add)
+
+        exp_out(0)
+        for t in range(PACK):
+            if t + 1 < PACK:
+                exp_out(t + 1)
+            if t > 0:
+                nc.scalar.activation(y_win[t][:, :S], banks[t][:], ACT.Copy, scale=0.5)
+            for a in (0, S // 2):
+                b = a + S // 2
+                nc.scalar.activation(second[:, t, a:b], y_win[t][:].indirect(n2_l[:, a // 16 : b // 16]), ACT.Exp)
+            if t + 1 < PACK:
+                sums(t, 0, S)
+            else:
+                sums(t, 0, S // 2)
+                sums(t, S // 2, S)
+            if t == 1:
+                nc.vector.tensor_copy(cs[:], xs[:].indirect(cand_l[:]))
+                cwd = deal("cwd", cw, I32)
+                csd = deal("csd", cs, U8)
+
+        zw = sb("zw", [P, S], I32)
+        zs = sb("zs", [P, S], U8)
+        for c, (a, b) in enumerate(Z_CHUNKS):
+            n = b - a
+            ln_num = sb("ln_num%d" % c, [P, PACK * n], F32)
+            ln_den = sb("ln_den%d" % c, [P, PACK * n], F32)
+            ratio = sb("ratio%d" % c, [P, n, PACK], F32)
+            zb = sb("zb%d" % c, [P, n, PACK], BF16)
+            nc.scalar.activation(interleaved(ln_num[:]), planar(num[:, :, a:b]), ACT.Ln)
+            nc.scalar.activation(interleaved(ln_den[:]), planar(den[:, :, a:b]), ACT.Ln)
+            nc.vector.tensor_tensor(ratio[:].rearrange("p n t -> p (n t)"), ln_num[:], ln_den[:], ALU.subtract)
+            nc.vector.tensor_tensor(zb[:], ratio[:], gain[:].unsqueeze(1).to_broadcast([P, n, PACK]), ALU.mult)
+            nc.vector.quantize_mx(zw[:, a:b].bitcast(FP8X4), zs[:, a:b], zb[:].rearrange("p n t -> p (n t)"))
+            for t in range(PACK):
+                if b <= EARLY:
+                    product(banks[t][:, a:b], cwd, csd, t, zw[:, a:b], zs[:, a:b])
+                else:
+                    product(banks[4 + t][:, a:b], cwd, csd, t, zw[:, a:b], zs[:, a:b])
+
+        s_plain = sb("s_plain", [P, PACK, S], F32)
+        st = [sb("st%d" % t, [P, S], F32) for t in range(PACK)]
+        for t in range(PACK):
+            for bank, a, b in ((banks[t], 0, EARLY), (banks[4 + t], EARLY, S)):
+                nc.scalar.activation(ex_win[t][:, a:b], bank[:, a:b], ACT.Copy, scale=-0.0625)
+                nc.scalar.activation(s_plain[:, t, a:b], bank[:, a:b], ACT.Copy, scale=0.0625)
+            nc.vector.tensor_tensor(st[t][:], ex_win[t][:].indirect(n4_l[:]), s_plain[:, t, :], ALU.add)
+
+        ow = sb("ow", [P, S], I32)
+        osc = sb("osc", [P, S], U8)
+        out_rows = out_0.rearrange("(p t) j -> p t j", t=PACK)
+        out_words = out_1[0].rearrange("p n r -> p (n r)").bitcast(I32)
+        for c, (a, b) in enumerate(OUT_CHUNKS):
+            n = b - a
+            other = sb("other%d" % c, [P, PACK, n], F32)
+            res = sb("res%d" % c, [P, PACK, n], F32)
+            rb = sb("rb%d" % c, [P, PACK * n], BF16)
+            for t in range(PACK):
+                nc.vector.tensor_copy(other[:, t, :], st[t][:].indirect(n5_l[:, a // 16 : b // 16]))
+            for t in range(PACK):
+                nc.vector.tensor_tensor(res[:, t, :], other[:, t, :], st[t][:, a:b], ALU.max)
+            nc.sync.dma_start(out_rows[:, :, a:b], res[:])
+            if b < S:
+                nc.scalar.copy(interleaved(rb[:]), planar(res[:]))
+            else:
+                nc.vector.tensor_copy(interleaved(rb[:]), planar(res[:]))
+            nc.vector.quantize_mx(ow[:, a:b].bitcast(FP8X4), osc[:, a:b], rb[:])
+            nc.sync.dma_start(out_words[:, a:b], ow[:, a:b])
+        for q in range(4):
+            queue = nc.sync if q % 2 == 0 else nc.scalar
+            queue.dma_start(out_2[0, 4 * q : 4 * q + 4, :].bitcast(I32), osc[32 * q : 32 * q + 4, :].bitcast(I32))

@@ -19,8 +19,9 @@ PACK = 4
 T = 2048
 S = 512
 WIN = 1024
-Z_CHUNKS = ((0, 128), (128, 256), (256, 384), (384, 512))
-EARLY = 384
+HALF = S // 2
+Z_CHUNKS = ((0, 64), (64, 128), (128, 256), (256, 384), (384, 512))
+FIRST_TILE_PARTS = ((0, 256), (256, 384), (384, 512))
 OUT_CHUNKS = ((0, 256), (256, 384), (384, 512))
 
 
@@ -30,8 +31,8 @@ def tile_picked_candoddshopmx_none_po_kernel(tc, x_words, x_scales, w1_words, w1
         held = ctx.enter_context(tc.tile_pool(name="held", bufs=1))
         psum = ctx.enter_context(tc.psum_pool(name="psum", bufs=1))
 
-        def sb(name, shape, dtype):
-            return held.tile(shape, dtype, name=name, align_bytes=64)
+        def sb(name, shape, dtype, tag=None):
+            return held.tile(shape, dtype, name=name, tag=tag or name, align_bytes=64)
 
         def load_list(name, src):
             tile = sb(name, [P, S // 16], U16)
@@ -52,7 +53,11 @@ def tile_picked_candoddshopmx_none_po_kernel(tc, x_words, x_scales, w1_words, w1
 
         def deal(name, src, dtype):
             tile = sb(name, [P, S], dtype)
-            nc.vector.tensor_copy(tile[:].rearrange("p (t m) -> p m t", t=PACK), src[:].rearrange("p (m t) -> p m t", t=PACK))
+            run = 4 if dtype == I32 else P
+            nc.vector.tensor_copy(
+                tile[:].rearrange("p (t c i) -> p c t i", t=PACK, i=run),
+                src[:].rearrange("p (c i t) -> p c t i", t=PACK, i=run),
+            )
             return tile
 
         def window(name):
@@ -72,76 +77,66 @@ def tile_picked_candoddshopmx_none_po_kernel(tc, x_words, x_scales, w1_words, w1
             )
 
         def interleaved(ap):
-            return ap.rearrange("p (c i t) -> p c t i", i=4, t=PACK)
+            return ap.rearrange("p (c i t) -> p c t i", i=2, t=PACK)
 
         def planar(ap):
-            return ap.rearrange("p t (c i) -> p c t i", i=4)
+            return ap.rearrange("p t (c i) -> p c t i", i=2)
+
+        def cols(h):
+            return slice(h * HALF, (h + 1) * HALF)
+
+        def entries(lst, h):
+            return lst[:, h * HALF // 16 : (h + 1) * HALF // 16]
 
         offs_l = load_list("offs_l", offs)
         ww = load_words("ww", w1_words, S, nc.scalar)
+        n1_l = load_list("n1_l", n1)
         xs = load_scales("xs", x_scales, T, (nc.sync, nc.sync, nc.scalar, nc.scalar))
         xw = load_words("xw", x_words, T, nc.sync)
+        s_win = [window("s_win%d" % t) for t in range(PACK)]
         ws = load_scales("ws", w1_scales, S, (nc.scalar,) * 4)
-        cand_l = load_list("cand_l", cand)
-        n1_l = load_list("n1_l", n1)
         n2_l = load_list("n2_l", n2)
         n3_l = load_list("n3_l", n3)
+        cand_l = load_list("cand_l", cand)
         gain = sb("gain", [P, PACK], F32)
         nc.sync.dma_start(gain[:], gs.rearrange("(p t) o -> p (t o)", t=PACK))
         n4_l = load_list("n4_l", n4)
         n5_l = load_list("n5_l", n5)
 
-        ex_win = [window("ex_win%d" % t) for t in range(PACK)]
+        ex_win = [sb("ex_win%d" % t, [P, S], F32) for t in range(PACK)]
         y_win = [sb("y_win%d" % t, [P, S], F32) for t in range(PACK)]
         banks = [psum.tile([P, S], F32, name="bank%d" % b) for b in range(8)]
 
         wwd = deal("wwd", ww, I32)
         qw = sb("qw", [P, S], I32)
         qs = sb("qs", [P, S], U8)
-        cw = sb("cw", [P, S], I32)
-        cs = sb("cs", [P, S], U8)
         nc.vector.tensor_copy(qw[:].bitcast(U32), xw[:].bitcast(U32).indirect(offs_l[:]))
         nc.vector.tensor_copy(qs[:], xs[:].indirect(offs_l[:]))
         wsd = deal("wsd", ws, U8)
         for t in range(PACK):
             product(banks[t][:], wwd, wsd, t, qw[:], qs[:])
+        cw = sb("cw", [P, S], I32, tag="ws")
+        cs = sb("cs", [P, S], U8)
         nc.vector.tensor_copy(cw[:].bitcast(U32), xw[:].bitcast(U32).indirect(cand_l[:]))
+        nc.vector.tensor_copy(cs[:], xs[:].indirect(cand_l[:]))
+        cwd = deal("cwd", cw, I32)
+        csd = deal("csd", cs, U8)
 
-        ex_plain = sb("ex_plain", [P, PACK, S], F32)
-        second = sb("second", [P, PACK, S], F32)
-        num = sb("num", [P, PACK, S], F32)
-        den = sb("den", [P, PACK, S], F32)
-
-        def exp_out(t):
-            nc.scalar.activation(ex_win[t][:, :S], banks[t][:], ACT.Exp, scale=0.5)
-            if t == 0:
-                nc.vector.tensor_scalar(y_win[t][:, :S], banks[t][:], 0.5, None, ALU.mult)
-                nc.vector.tensor_copy(ex_plain[:, t, :], ex_win[t][:, :S])
-            else:
-                nc.sync.dma_start(ex_plain[:, t, :], ex_win[t][:, :S])
-
-        def sums(t, a, b):
-            nc.vector.tensor_tensor(num[:, t, a:b], ex_win[t][:].indirect(n1_l[:, a // 16 : b // 16]), ex_plain[:, t, a:b], ALU.add)
-            nc.vector.tensor_tensor(den[:, t, a:b], ex_win[t][:].indirect(n3_l[:, a // 16 : b // 16]), second[:, t, a:b], ALU.add)
-
-        exp_out(0)
+        second = [sb("second%d" % t, [P, S], F32) for t in range(PACK)]
+        num = [sb("num%d" % h, [P, PACK, HALF], F32) for h in range(2)]
+        den = [sb("den%d" % h, [P, PACK, HALF], F32) for h in range(2)]
+        ex_last = sb("ex_last", [P, S], F32)
         for t in range(PACK):
-            if t + 1 < PACK:
-                exp_out(t + 1)
-            if t > 0:
-                nc.scalar.activation(y_win[t][:, :S], banks[t][:], ACT.Copy, scale=0.5)
-            for a in (0, S // 2):
-                b = a + S // 2
-                nc.scalar.activation(second[:, t, a:b], y_win[t][:].indirect(n2_l[:, a // 16 : b // 16]), ACT.Exp)
-            if t + 1 < PACK:
-                sums(t, 0, S)
-            else:
-                sums(t, 0, S // 2)
-                sums(t, S // 2, S)
-            if t == 1:
-                nc.vector.tensor_copy(cs[:], xs[:].indirect(cand_l[:]))
-                cwd = deal("cwd", cw, I32)
-                csd = deal("csd", cs, U8)
+            ex_plain = [den[h][:, t + 1, :] if t + 1 < PACK else ex_last[:, cols(h)] for h in range(2)]
+            nc.scalar.activation(ex_win[t][:], banks[t][:], ACT.Exp, scale=0.5)
+            for h in range(2):
+                nc.sync.dma_start(ex_plain[h], ex_win[t][:, cols(h)])
+            nc.scalar.activation(y_win[t][:], banks[t][:], ACT.Copy, scale=0.5)
+            for h in range(2):
+                nc.scalar.activation(second[t][:, cols(h)], y_win[t][:].indirect(entries(n2_l, h)), ACT.Exp)
+            for h in range(2):
+                nc.vector.tensor_tensor(den[h][:, t, :], ex_win[t][:].indirect(entries(n3_l, h)), second[t][:, cols(h)], ALU.add)
+                nc.vector.tensor_tensor(num[h][:, t, :], ex_win[t][:].indirect(entries(n1_l, h)), ex_plain[h], ALU.add)
 
         zw = sb("zw", [P, S], I32)
         zs = sb("zs", [P, S], U8)
@@ -151,24 +146,21 @@ def tile_picked_candoddshopmx_none_po_kernel(tc, x_words, x_scales, w1_words, w1
             ln_den = sb("ln_den%d" % c, [P, PACK * n], F32)
             ratio = sb("ratio%d" % c, [P, n, PACK], F32)
             zb = sb("zb%d" % c, [P, n, PACK], BF16)
-            nc.scalar.activation(interleaved(ln_num[:]), planar(num[:, :, a:b]), ACT.Ln)
-            nc.scalar.activation(interleaved(ln_den[:]), planar(den[:, :, a:b]), ACT.Ln)
+            nc.scalar.activation(interleaved(ln_num[:]), planar(num[a // HALF][:, :, a % HALF : a % HALF + n]), ACT.Ln)
+            nc.scalar.activation(interleaved(ln_den[:]), planar(den[a // HALF][:, :, a % HALF : a % HALF + n]), ACT.Ln)
             nc.vector.tensor_tensor(ratio[:].rearrange("p n t -> p (n t)"), ln_num[:], ln_den[:], ALU.subtract)
             nc.vector.tensor_tensor(zb[:], ratio[:], gain[:].unsqueeze(1).to_broadcast([P, n, PACK]), ALU.mult)
             nc.vector.quantize_mx(zw[:, a:b].bitcast(FP8X4), zs[:, a:b], zb[:].rearrange("p n t -> p (n t)"))
-            for t in range(PACK):
-                if b <= EARLY:
-                    product(banks[t][:, a:b], cwd, csd, t, zw[:, a:b], zs[:, a:b])
-                else:
-                    product(banks[4 + t][:, a:b], cwd, csd, t, zw[:, a:b], zs[:, a:b])
 
-        s_plain = sb("s_plain", [P, PACK, S], F32)
+        s_plain = [sb("s_plain%d" % t, [P, S], F32) for t in range(PACK)]
         st = [sb("st%d" % t, [P, S], F32) for t in range(PACK)]
         for t in range(PACK):
-            for bank, a, b in ((banks[t], 0, EARLY), (banks[4 + t], EARLY, S)):
-                nc.scalar.activation(ex_win[t][:, a:b], bank[:, a:b], ACT.Copy, scale=-0.0625)
-                nc.scalar.activation(s_plain[:, t, a:b], bank[:, a:b], ACT.Copy, scale=0.0625)
-            nc.vector.tensor_tensor(st[t][:], ex_win[t][:].indirect(n4_l[:]), s_plain[:, t, :], ALU.add)
+            for i, (a, b) in enumerate(FIRST_TILE_PARTS if t == 0 else ((0, S),)):
+                bank = banks[4 + i] if t == 0 else banks[t]
+                product(bank[:, a:b], cwd, csd, t, zw[:, a:b], zs[:, a:b])
+                nc.scalar.activation(s_win[t][:, a:b], bank[:, a:b], ACT.Copy, scale=-0.0625)
+                nc.scalar.activation(s_plain[t][:, a:b], bank[:, a:b], ACT.Copy, scale=0.0625)
+            nc.vector.tensor_tensor(st[t][:], s_win[t][:].indirect(n4_l[:]), s_plain[t][:], ALU.add)
 
         ow = sb("ow", [P, S], I32)
         osc = sb("osc", [P, S], U8)
@@ -176,7 +168,7 @@ def tile_picked_candoddshopmx_none_po_kernel(tc, x_words, x_scales, w1_words, w1
         out_words = out_1[0].rearrange("p n r -> p (n r)").bitcast(I32)
         for c, (a, b) in enumerate(OUT_CHUNKS):
             n = b - a
-            other = sb("other%d" % c, [P, PACK, n], F32)
+            other = sb("other%d" % c, [P, PACK, n], F32, tag=("s_win3", "s_plain3")[c % 2])
             res = sb("res%d" % c, [P, PACK, n], F32)
             rb = sb("rb%d" % c, [P, PACK * n], BF16)
             for t in range(PACK):

@@ -1,6 +1,7 @@
 from contextlib import ExitStack
 
 import concourse.mybir as mybir
+from concourse.masks import make_identity
 
 FLOPS = 2 * 512 * 512 * 512 * 2
 
@@ -21,7 +22,7 @@ S = 512
 WIN = 1024
 HALF = S // 2
 Z_CHUNKS = ((0, 64), (64, 128), (128, 256), (256, 384), (384, 512))
-FIRST_TILE_PARTS = ((0, 256), (256, 384), (384, 512))
+SCORE_PARTS = (((0, 256, 4), (256, 384, 5), (384, 512, 6)), ((0, 256, 1), (256, 512, 7)), ((0, 512, 2),), ((0, 512, 3),))
 OUT_CHUNKS = ((0, 256), (256, 384), (384, 512))
 
 
@@ -51,12 +52,12 @@ def tile_picked_candoddshopmx_none_po_kernel(tc, x_words, x_scales, w1_words, w1
             queue.dma_start(tile[:], src[0].rearrange("p n r -> p (n r)").bitcast(I32))
             return tile
 
-        def deal(name, src, dtype):
-            tile = sb(name, [P, S], dtype)
+        def deal(name, src, dtype, engine, first, count, tag=None):
+            tile = sb(name, [P, count * P], dtype, tag=tag)
             run = 4 if dtype == I32 else P
-            nc.vector.tensor_copy(
-                tile[:].rearrange("p (t c i) -> p c t i", t=PACK, i=run),
-                src[:].rearrange("p (c i t) -> p c t i", t=PACK, i=run),
+            engine.tensor_copy(
+                tile[:].rearrange("p (t c i) -> p c t i", t=count, i=run),
+                src[:].rearrange("p (c i t) -> p c t i", t=PACK, i=run)[:, :, first : first + count, :],
             )
             return tile
 
@@ -107,20 +108,20 @@ def tile_picked_candoddshopmx_none_po_kernel(tc, x_words, x_scales, w1_words, w1
         y_win = [sb("y_win%d" % t, [P, S], F32) for t in range(PACK)]
         banks = [psum.tile([P, S], F32, name="bank%d" % b) for b in range(8)]
 
-        wwd = deal("wwd", ww, I32)
+        wwd = deal("wwd", ww, I32, nc.vector, 0, PACK)
         qw = sb("qw", [P, S], I32)
         qs = sb("qs", [P, S], U8)
         nc.vector.tensor_copy(qw[:].bitcast(U32), xw[:].bitcast(U32).indirect(offs_l[:]))
         nc.vector.tensor_copy(qs[:], xs[:].indirect(offs_l[:]))
-        wsd = deal("wsd", ws, U8)
+        wsd = deal("wsd", ws, U8, nc.gpsimd, 0, PACK)
         for t in range(PACK):
             product(banks[t][:], wwd, wsd, t, qw[:], qs[:])
-        cw = sb("cw", [P, S], I32, tag="ws")
+        cw = sb("cw", [P, S], I32)
         cs = sb("cs", [P, S], U8)
         nc.vector.tensor_copy(cw[:].bitcast(U32), xw[:].bitcast(U32).indirect(cand_l[:]))
         nc.vector.tensor_copy(cs[:], xs[:].indirect(cand_l[:]))
-        cwd = deal("cwd", cw, I32)
-        csd = deal("csd", cs, U8)
+        cwd = [deal("cwd0", cw, I32, nc.vector, 0, 2)]
+        csd = [deal("csd0", cs, U8, nc.vector, 0, 2)]
 
         second = [sb("second%d" % t, [P, S], F32) for t in range(PACK)]
         num = [sb("num%d" % h, [P, PACK, HALF], F32) for h in range(2)]
@@ -131,7 +132,10 @@ def tile_picked_candoddshopmx_none_po_kernel(tc, x_words, x_scales, w1_words, w1
             nc.scalar.activation(ex_win[t][:], banks[t][:], ACT.Exp, scale=0.5)
             for h in range(2):
                 nc.sync.dma_start(ex_plain[h], ex_win[t][:, cols(h)])
-            nc.scalar.activation(y_win[t][:], banks[t][:], ACT.Copy, scale=0.5)
+            if t == 1:
+                nc.vector.tensor_scalar(y_win[t][:], banks[t][:], 0.5, None, ALU.mult)
+            else:
+                nc.scalar.activation(y_win[t][:], banks[t][:], ACT.Copy, scale=0.5)
             for h in range(2):
                 nc.scalar.activation(second[t][:, cols(h)], y_win[t][:].indirect(entries(n2_l, h)), ACT.Exp)
             for h in range(2):
@@ -152,15 +156,69 @@ def tile_picked_candoddshopmx_none_po_kernel(tc, x_words, x_scales, w1_words, w1
             nc.vector.tensor_tensor(zb[:], ratio[:], gain[:].unsqueeze(1).to_broadcast([P, n, PACK]), ALU.mult)
             nc.vector.quantize_mx(zw[:, a:b].bitcast(FP8X4), zs[:, a:b], zb[:].rearrange("p n t -> p (n t)"))
 
+        last = len(Z_CHUNKS) - 1
+        csd.append(deal("csd1", cs, U8, nc.vector, 2, 2, tag="ratio%d" % last))
+        cwd.append(deal("cwd1", cw, I32, nc.vector, 2, 2, tag="zb%d" % last))
+
         s_plain = [sb("s_plain%d" % t, [P, S], F32) for t in range(PACK)]
-        st = [sb("st%d" % t, [P, S], F32) for t in range(PACK)]
-        for t in range(PACK):
-            for i, (a, b) in enumerate(FIRST_TILE_PARTS if t == 0 else ((0, S),)):
-                bank = banks[4 + i] if t == 0 else banks[t]
-                product(bank[:, a:b], cwd, csd, t, zw[:, a:b], zs[:, a:b])
+        st = {}
+        res = [sb("res%d" % c, [P, PACK, b - a], F32) for c, (a, b) in enumerate(OUT_CHUNKS)]
+        st_plain = [sb("st_plain%d" % t, [P, S], F32) for t in range(2)]
+        excess = [sb("excess%d" % t, [P, S], F32) for t in range(2)]
+        lift = [sb("lift%d" % t, [P, S], F32) for t in range(2)]
+        turned = [sb("turned%d" % t, [P, S], F32) for t in range(2)]
+        ident = sb("ident", [P, P], F32)
+        make_identity(nc, ident[:])
+
+        def scores(t):
+            for a, b, which in SCORE_PARTS[t]:
+                bank = banks[which]
+                product(bank[:, a:b], cwd[t // 2], csd[t // 2], t % 2, zw[:, a:b], zs[:, a:b])
                 nc.scalar.activation(s_win[t][:, a:b], bank[:, a:b], ACT.Copy, scale=-0.0625)
                 nc.scalar.activation(s_plain[t][:, a:b], bank[:, a:b], ACT.Copy, scale=0.0625)
+
+        def step(t):
+            st[t] = sb("st%d" % t, [P, S], F32, tag="st_plain1" if t == 2 else None)
             nc.vector.tensor_tensor(st[t][:], s_win[t][:].indirect(n4_l[:]), s_plain[t][:], ALU.add)
+
+        def differ(t):
+            nc.scalar.copy(st_plain[t][:], st[t][:])
+            for h in range(2):
+                nc.vector.tensor_tensor(excess[t][:, cols(h)], st[t][:].indirect(entries(n5_l, h)), st_plain[t][:, cols(h)], ALU.subtract)
+
+        def lifted(t):
+            nc.scalar.activation(lift[t][:], excess[t][:], ACT.Relu)
+
+        def turn(t):
+            bank = banks[(0, 4)[t]]
+            for j in range(0, S, P):
+                nc.tensor.matmul(bank[:, j : j + P], st[t][:, j : j + P], ident[:], start=True, stop=False, is_transpose=True)
+                nc.tensor.matmul(bank[:, j : j + P], lift[t][:, j : j + P], ident[:], start=False, stop=True, is_transpose=True)
+            nc.scalar.copy(turned[t][:], bank[:])
+
+        def turn_back(t):
+            bank = banks[5 + t]
+            for j in range(0, S, P):
+                nc.tensor.transpose(bank[:, j : j + P], turned[t][:, j : j + P], ident[:])
+            for c, (a, b) in enumerate(OUT_CHUNKS):
+                nc.scalar.copy(res[c][:, t, :], bank[:, a:b])
+
+        scores(0)
+        step(0)
+        scores(1)
+        step(1)
+        differ(0)
+        scores(2)
+        differ(1)
+        lifted(0)
+        scores(3)
+        step(2)
+        lifted(1)
+        step(3)
+        turn(0)
+        turn(1)
+        turn_back(0)
+        turn_back(1)
 
         ow = sb("ow", [P, S], I32)
         osc = sb("osc", [P, S], U8)
@@ -168,20 +226,21 @@ def tile_picked_candoddshopmx_none_po_kernel(tc, x_words, x_scales, w1_words, w1
         out_words = out_1[0].rearrange("p n r -> p (n r)").bitcast(I32)
         for c, (a, b) in enumerate(OUT_CHUNKS):
             n = b - a
-            other = sb("other%d" % c, [P, PACK, n], F32, tag=("s_win3", "s_plain3")[c % 2])
-            res = sb("res%d" % c, [P, PACK, n], F32)
+            other = sb("other%d" % c, [P, 2, n], F32, tag=("s_win3", "s_plain3")[c % 2])
             rb = sb("rb%d" % c, [P, PACK * n], BF16)
-            for t in range(PACK):
-                nc.vector.tensor_copy(other[:, t, :], st[t][:].indirect(n5_l[:, a // 16 : b // 16]))
-            for t in range(PACK):
-                nc.vector.tensor_tensor(res[:, t, :], other[:, t, :], st[t][:, a:b], ALU.max)
-            nc.sync.dma_start(out_rows[:, :, a:b], res[:])
+            for t in (2, 3):
+                nc.vector.tensor_copy(other[:, t - 2, :], st[t][:].indirect(n5_l[:, a // 16 : b // 16]))
+            for t in (2, 3):
+                nc.vector.tensor_tensor(res[c][:, t, :], other[:, t - 2, :], st[t][:, a:b], ALU.max)
+            nc.sync.dma_start(out_rows[:, :, a:b], res[c][:])
             if b < S:
-                nc.scalar.copy(interleaved(rb[:]), planar(res[:]))
+                nc.scalar.copy(interleaved(rb[:]), planar(res[c][:]))
             else:
-                nc.vector.tensor_copy(interleaved(rb[:]), planar(res[:]))
+                nc.vector.tensor_copy(interleaved(rb[:]), planar(res[c][:]))
             nc.vector.quantize_mx(ow[:, a:b].bitcast(FP8X4), osc[:, a:b], rb[:])
-            nc.sync.dma_start(out_words[:, a:b], ow[:, a:b])
+            if c != 1:
+                first = min(a, HALF)
+                nc.sync.dma_start(out_words[:, first:b], ow[:, first:b])
         for q in range(4):
             queue = nc.sync if q % 2 == 0 else nc.scalar
             queue.dma_start(out_2[0, 4 * q : 4 * q + 4, :].bitcast(I32), osc[32 * q : 32 * q + 4, :].bitcast(I32))

@@ -17,34 +17,50 @@ ALU = mybir.AluOpType
 
 P = 128
 PACK = 4
+QUADRANTS = 4
+PER_COLUMN = 16
 T = 2048
 S = 512
-WIN = 1024
 HALF = S // 2
+SCORE_SCALE = 0.0625
+
+Y_TILE_ON_VECTOR = 1
 Z_CHUNKS = ((0, 64), (64, 128), (128, 256), (256, 384), (384, 512))
-SCORE_PARTS = (((0, 256, 4), (256, 384, 5), (384, 512, 6)), ((0, 256, 1), (256, 512, 7)), ((0, 512, 2),), ((0, 512, 3),))
+SCORE_PARTS = (
+    ((0, 256, 4), (256, 384, 5), (384, 512, 6)),
+    ((0, 256, 1), (256, 512, 7)),
+    ((0, 512, 2),),
+    ((0, 512, 3),),
+)
+SUM_TILES = (0, 1)
+SUM_BANKS = (0, 4)
+BACK_BANKS = (5, 6)
 OUT_CHUNKS = ((0, 256), (256, 384), (384, 512))
 
 
-def tile_picked_candoddshopmx_none_po_kernel(tc, x_words, x_scales, w1_words, w1_scales, gs, offs, n1, n2, n3, cand, n4, n5, out_0, out_1, out_2):
+def tile_picked_candoddshopmx_none_po_kernel(
+    tc, x_words, x_scales, w1_words, w1_scales, gs, offs, n1, n2, n3, cand, n4, n5, out_0, out_1, out_2
+):
     nc = tc.nc
     with ExitStack() as ctx:
         held = ctx.enter_context(tc.tile_pool(name="held", bufs=1))
         psum = ctx.enter_context(tc.psum_pool(name="psum", bufs=1))
 
-        def sb(name, shape, dtype, tag=None):
-            return held.tile(shape, dtype, name=name, tag=tag or name, align_bytes=64)
+        def sb(name, shape, dtype, after=None):
+            return held.tile(shape, dtype, name=name, tag=after or name, align_bytes=64)
 
         def load_list(name, src):
-            tile = sb(name, [P, S // 16], U16)
+            tile = sb(name, [P, S // PER_COLUMN], U16)
             nc.sync.dma_start(tile[:], src)
             return tile
 
         def load_scales(name, src, width, queues):
             tile = sb(name, [P, width], U8)
             nc.vector.memset(tile[:].bitcast(I32), 0)
-            for q in range(4):
-                queues[q].dma_start(tile[32 * q : 32 * q + 4, :].bitcast(I32), src[0, 4 * q : 4 * q + 4, :].bitcast(I32))
+            for q in range(QUADRANTS):
+                queues[q].dma_start(
+                    tile[32 * q : 32 * q + 4, :].bitcast(I32), src[0, 4 * q : 4 * q + 4, :].bitcast(I32)
+                )
             return tile
 
         def load_words(name, src, width, queue):
@@ -52,8 +68,8 @@ def tile_picked_candoddshopmx_none_po_kernel(tc, x_words, x_scales, w1_words, w1
             queue.dma_start(tile[:], src[0].rearrange("p n r -> p (n r)").bitcast(I32))
             return tile
 
-        def deal(name, src, dtype, engine, first, count, tag=None):
-            tile = sb(name, [P, count * P], dtype, tag=tag)
+        def deal(name, src, dtype, engine, first, count, after=None):
+            tile = sb(name, [P, count * P], dtype, after)
             run = 4 if dtype == I32 else P
             engine.tensor_copy(
                 tile[:].rearrange("p (t c i) -> p c t i", t=count, i=run),
@@ -61,16 +77,16 @@ def tile_picked_candoddshopmx_none_po_kernel(tc, x_words, x_scales, w1_words, w1
             )
             return tile
 
-        def window(name):
-            tile = sb(name, [P, WIN], F32)
+        def wide_window(name):
+            tile = sb(name, [P, 2 * S], F32)
             nc.vector.memset(tile[:, S:], 0.0)
             return tile
 
-        def product(out, words, scales, t, rhs_words, rhs_scales):
+        def product(out, words, scales, block, rhs_words, rhs_scales):
             nc.tensor.matmul_mx(
                 out,
-                lhsT=words[:, P * t : P * (t + 1)].bitcast(FP8X4),
-                lhsT_scale=scales[:, P * t : P * (t + 1)],
+                lhsT=words[:, P * block : P * (block + 1)].bitcast(FP8X4),
+                lhsT_scale=scales[:, P * block : P * (block + 1)],
                 rhs=rhs_words.bitcast(FP8X4),
                 rhs_scale=rhs_scales,
                 start=True,
@@ -83,164 +99,193 @@ def tile_picked_candoddshopmx_none_po_kernel(tc, x_words, x_scales, w1_words, w1
         def planar(ap):
             return ap.rearrange("p t (c i) -> p c t i", i=2)
 
-        def cols(h):
+        def half(h):
             return slice(h * HALF, (h + 1) * HALF)
 
-        def entries(lst, h):
-            return lst[:, h * HALF // 16 : (h + 1) * HALF // 16]
+        def entries(list_tile, a, b):
+            return list_tile[:, a // PER_COLUMN : b // PER_COLUMN]
 
-        offs_l = load_list("offs_l", offs)
-        ww = load_words("ww", w1_words, S, nc.scalar)
-        n1_l = load_list("n1_l", n1)
-        xs = load_scales("xs", x_scales, T, (nc.sync, nc.sync, nc.scalar, nc.scalar))
-        xw = load_words("xw", x_words, T, nc.sync)
-        s_win = [window("s_win%d" % t) for t in range(PACK)]
-        ws = load_scales("ws", w1_scales, S, (nc.scalar,) * 4)
-        n2_l = load_list("n2_l", n2)
-        n3_l = load_list("n3_l", n3)
-        cand_l = load_list("cand_l", cand)
+        def half_entries(list_tile, h):
+            return entries(list_tile, h * HALF, (h + 1) * HALF)
+
+        offs_list = load_list("offs_list", offs)
+        w_words = load_words("w_words", w1_words, S, nc.scalar)
+        n1_list = load_list("n1_list", n1)
+        table_scales = load_scales("table_scales", x_scales, T, (nc.sync, nc.sync, nc.scalar, nc.scalar))
+        table_words = load_words("table_words", x_words, T, nc.sync)
+        neg_s = [wide_window("neg_s%d" % t) for t in range(PACK)]
+        w_scales = load_scales("w_scales", w1_scales, S, (nc.scalar,) * QUADRANTS)
+        n2_list = load_list("n2_list", n2)
+        n3_list = load_list("n3_list", n3)
+        cand_list = load_list("cand_list", cand)
         gain = sb("gain", [P, PACK], F32)
         nc.sync.dma_start(gain[:], gs.rearrange("(p t) o -> p (t o)", t=PACK))
-        n4_l = load_list("n4_l", n4)
-        n5_l = load_list("n5_l", n5)
+        n4_list = load_list("n4_list", n4)
+        n5_list = load_list("n5_list", n5)
 
-        ex_win = [sb("ex_win%d" % t, [P, S], F32) for t in range(PACK)]
-        y_win = [sb("y_win%d" % t, [P, S], F32) for t in range(PACK)]
+        ex = [sb("ex%d" % t, [P, S], F32) for t in range(PACK)]
+        half_y = [sb("half_y%d" % t, [P, S], F32) for t in range(PACK)]
         banks = [psum.tile([P, S], F32, name="bank%d" % b) for b in range(8)]
 
-        wwd = deal("wwd", ww, I32, nc.vector, 0, PACK)
-        qw = sb("qw", [P, S], I32)
-        qs = sb("qs", [P, S], U8)
-        nc.vector.tensor_copy(qw[:].bitcast(U32), xw[:].bitcast(U32).indirect(offs_l[:]))
-        nc.vector.tensor_copy(qs[:], xs[:].indirect(offs_l[:]))
-        wsd = deal("wsd", ws, U8, nc.gpsimd, 0, PACK)
+        w_words_dealt = deal("w_words_dealt", w_words, I32, nc.vector, 0, PACK)
+        pick_words = sb("pick_words", [P, S], I32)
+        pick_scales = sb("pick_scales", [P, S], U8)
+        nc.vector.tensor_copy(pick_words[:].bitcast(U32), table_words[:].bitcast(U32).indirect(offs_list[:]))
+        nc.vector.tensor_copy(pick_scales[:], table_scales[:].indirect(offs_list[:]))
+        w_scales_dealt = deal("w_scales_dealt", w_scales, U8, nc.gpsimd, 0, PACK)
         for t in range(PACK):
-            product(banks[t][:], wwd, wsd, t, qw[:], qs[:])
-        cw = sb("cw", [P, S], I32)
-        cs = sb("cs", [P, S], U8)
-        nc.vector.tensor_copy(cw[:].bitcast(U32), xw[:].bitcast(U32).indirect(cand_l[:]))
-        nc.vector.tensor_copy(cs[:], xs[:].indirect(cand_l[:]))
-        cwd = [deal("cwd0", cw, I32, nc.vector, 0, 2)]
-        csd = [deal("csd0", cs, U8, nc.vector, 0, 2)]
+            product(banks[t][:], w_words_dealt, w_scales_dealt, t, pick_words[:], pick_scales[:])
 
-        second = [sb("second%d" % t, [P, S], F32) for t in range(PACK)]
+        cand_words = sb("cand_words", [P, S], I32)
+        cand_scales = sb("cand_scales", [P, S], U8)
+        nc.vector.tensor_copy(cand_words[:].bitcast(U32), table_words[:].bitcast(U32).indirect(cand_list[:]))
+        nc.vector.tensor_copy(cand_scales[:], table_scales[:].indirect(cand_list[:]))
+        cand_words_dealt = [deal("cand_words_dealt0", cand_words, I32, nc.vector, 0, 2)]
+        cand_scales_dealt = [deal("cand_scales_dealt0", cand_scales, U8, nc.vector, 0, 2)]
+
+        ex_n2 = [sb("ex_n2_%d" % t, [P, S], F32) for t in range(PACK)]
         num = [sb("num%d" % h, [P, PACK, HALF], F32) for h in range(2)]
         den = [sb("den%d" % h, [P, PACK, HALF], F32) for h in range(2)]
-        ex_last = sb("ex_last", [P, S], F32)
+        ex_copy_last = sb("ex_copy_last", [P, S], F32)
         for t in range(PACK):
-            ex_plain = [den[h][:, t + 1, :] if t + 1 < PACK else ex_last[:, cols(h)] for h in range(2)]
-            nc.scalar.activation(ex_win[t][:], banks[t][:], ACT.Exp, scale=0.5)
+            ex_copy = [den[h][:, t + 1, :] if t + 1 < PACK else ex_copy_last[:, half(h)] for h in range(2)]
+            nc.scalar.activation(ex[t][:], banks[t][:], ACT.Exp, scale=0.5)
             for h in range(2):
-                nc.sync.dma_start(ex_plain[h], ex_win[t][:, cols(h)])
-            if t == 1:
-                nc.vector.tensor_scalar(y_win[t][:], banks[t][:], 0.5, None, ALU.mult)
+                nc.sync.dma_start(ex_copy[h], ex[t][:, half(h)])
+            if t == Y_TILE_ON_VECTOR:
+                nc.vector.tensor_scalar(half_y[t][:], banks[t][:], 0.5, None, ALU.mult)
             else:
-                nc.scalar.activation(y_win[t][:], banks[t][:], ACT.Copy, scale=0.5)
+                nc.scalar.activation(half_y[t][:], banks[t][:], ACT.Copy, scale=0.5)
             for h in range(2):
-                nc.scalar.activation(second[t][:, cols(h)], y_win[t][:].indirect(entries(n2_l, h)), ACT.Exp)
+                nc.scalar.activation(ex_n2[t][:, half(h)], half_y[t][:].indirect(half_entries(n2_list, h)), ACT.Exp)
             for h in range(2):
-                nc.vector.tensor_tensor(den[h][:, t, :], ex_win[t][:].indirect(entries(n3_l, h)), second[t][:, cols(h)], ALU.add)
-                nc.vector.tensor_tensor(num[h][:, t, :], ex_win[t][:].indirect(entries(n1_l, h)), ex_plain[h], ALU.add)
+                nc.vector.tensor_tensor(
+                    den[h][:, t, :], ex[t][:].indirect(half_entries(n3_list, h)), ex_n2[t][:, half(h)], ALU.add
+                )
+                nc.vector.tensor_tensor(
+                    num[h][:, t, :], ex[t][:].indirect(half_entries(n1_list, h)), ex_copy[h], ALU.add
+                )
 
-        zw = sb("zw", [P, S], I32)
-        zs = sb("zs", [P, S], U8)
+        z_words = sb("z_words", [P, S], I32)
+        z_scales = sb("z_scales", [P, S], U8)
         for c, (a, b) in enumerate(Z_CHUNKS):
             n = b - a
+            inside = slice(a % HALF, a % HALF + n)
             ln_num = sb("ln_num%d" % c, [P, PACK * n], F32)
             ln_den = sb("ln_den%d" % c, [P, PACK * n], F32)
-            ratio = sb("ratio%d" % c, [P, n, PACK], F32)
-            zb = sb("zb%d" % c, [P, n, PACK], BF16)
-            nc.scalar.activation(interleaved(ln_num[:]), planar(num[a // HALF][:, :, a % HALF : a % HALF + n]), ACT.Ln)
-            nc.scalar.activation(interleaved(ln_den[:]), planar(den[a // HALF][:, :, a % HALF : a % HALF + n]), ACT.Ln)
-            nc.vector.tensor_tensor(ratio[:].rearrange("p n t -> p (n t)"), ln_num[:], ln_den[:], ALU.subtract)
-            nc.vector.tensor_tensor(zb[:], ratio[:], gain[:].unsqueeze(1).to_broadcast([P, n, PACK]), ALU.mult)
-            nc.vector.quantize_mx(zw[:, a:b].bitcast(FP8X4), zs[:, a:b], zb[:].rearrange("p n t -> p (n t)"))
+            odds = sb("odds%d" % c, [P, n, PACK], F32)
+            z = sb("z%d" % c, [P, n, PACK], BF16)
+            nc.scalar.activation(interleaved(ln_num[:]), planar(num[a // HALF][:, :, inside]), ACT.Ln)
+            nc.scalar.activation(interleaved(ln_den[:]), planar(den[a // HALF][:, :, inside]), ACT.Ln)
+            nc.vector.tensor_tensor(odds[:].rearrange("p n t -> p (n t)"), ln_num[:], ln_den[:], ALU.subtract)
+            nc.vector.tensor_tensor(z[:], odds[:], gain[:].unsqueeze(1).to_broadcast([P, n, PACK]), ALU.mult)
+            nc.vector.quantize_mx(
+                z_words[:, a:b].bitcast(FP8X4), z_scales[:, a:b], z[:].rearrange("p n t -> p (n t)")
+            )
 
         last = len(Z_CHUNKS) - 1
-        csd.append(deal("csd1", cs, U8, nc.vector, 2, 2, tag="ratio%d" % last))
-        cwd.append(deal("cwd1", cw, I32, nc.vector, 2, 2, tag="zb%d" % last))
+        cand_scales_dealt.append(deal("cand_scales_dealt1", cand_scales, U8, nc.vector, 2, 2, "odds%d" % last))
+        cand_words_dealt.append(deal("cand_words_dealt1", cand_words, I32, nc.vector, 2, 2, "z%d" % last))
 
-        s_plain = [sb("s_plain%d" % t, [P, S], F32) for t in range(PACK)]
+        s = [sb("s%d" % t, [P, S], F32) for t in range(PACK)]
         st = {}
-        res = [sb("res%d" % c, [P, PACK, b - a], F32) for c, (a, b) in enumerate(OUT_CHUNKS)]
-        st_plain = [sb("st_plain%d" % t, [P, S], F32) for t in range(2)]
-        excess = [sb("excess%d" % t, [P, S], F32) for t in range(2)]
-        lift = [sb("lift%d" % t, [P, S], F32) for t in range(2)]
-        turned = [sb("turned%d" % t, [P, S], F32) for t in range(2)]
+        result = sb("result", [P, PACK, S], F32)
+        out_rows = out_0.rearrange("(p t) j -> p t j", t=PACK)
+        st_copy = [sb("st_copy%d" % t, [P, S], F32) for t in SUM_TILES]
+        excess = [sb("excess%d" % t, [P, S], F32) for t in SUM_TILES]
+        lift = [sb("lift%d" % t, [P, S], F32) for t in SUM_TILES]
+        turned = [sb("turned%d" % t, [P, S], F32) for t in SUM_TILES]
         ident = sb("ident", [P, P], F32)
         make_identity(nc, ident[:])
 
         def scores(t):
             for a, b, which in SCORE_PARTS[t]:
                 bank = banks[which]
-                product(bank[:, a:b], cwd[t // 2], csd[t // 2], t % 2, zw[:, a:b], zs[:, a:b])
-                nc.scalar.activation(s_win[t][:, a:b], bank[:, a:b], ACT.Copy, scale=-0.0625)
-                nc.scalar.activation(s_plain[t][:, a:b], bank[:, a:b], ACT.Copy, scale=0.0625)
+                product(
+                    bank[:, a:b],
+                    cand_words_dealt[t // 2],
+                    cand_scales_dealt[t // 2],
+                    t % 2,
+                    z_words[:, a:b],
+                    z_scales[:, a:b],
+                )
+                nc.scalar.activation(neg_s[t][:, a:b], bank[:, a:b], ACT.Copy, scale=-SCORE_SCALE)
+                nc.scalar.activation(s[t][:, a:b], bank[:, a:b], ACT.Copy, scale=SCORE_SCALE)
 
-        def step(t):
-            st[t] = sb("st%d" % t, [P, S], F32, tag="st_plain1" if t == 2 else None)
-            nc.vector.tensor_tensor(st[t][:], s_win[t][:].indirect(n4_l[:]), s_plain[t][:], ALU.add)
+        def less_n4(t, after=None):
+            st[t] = sb("st%d" % t, [P, S], F32, after)
+            nc.vector.tensor_tensor(st[t][:], neg_s[t][:].indirect(n4_list[:]), s[t][:], ALU.add)
 
-        def differ(t):
-            nc.scalar.copy(st_plain[t][:], st[t][:])
+        def excess_n5(t):
+            nc.scalar.copy(st_copy[t][:], st[t][:])
             for h in range(2):
-                nc.vector.tensor_tensor(excess[t][:, cols(h)], st[t][:].indirect(entries(n5_l, h)), st_plain[t][:, cols(h)], ALU.subtract)
+                nc.vector.tensor_tensor(
+                    excess[t][:, half(h)],
+                    st[t][:].indirect(half_entries(n5_list, h)),
+                    st_copy[t][:, half(h)],
+                    ALU.subtract,
+                )
 
-        def lifted(t):
+        def positive_part(t):
             nc.scalar.activation(lift[t][:], excess[t][:], ACT.Relu)
 
-        def turn(t):
-            bank = banks[(0, 4)[t]]
+        def sum_turned(t):
+            bank = banks[SUM_BANKS[t]]
             for j in range(0, S, P):
-                nc.tensor.matmul(bank[:, j : j + P], st[t][:, j : j + P], ident[:], start=True, stop=False, is_transpose=True)
-                nc.tensor.matmul(bank[:, j : j + P], lift[t][:, j : j + P], ident[:], start=False, stop=True, is_transpose=True)
+                block = slice(j, j + P)
+                nc.tensor.matmul(bank[:, block], st[t][:, block], ident[:], start=True, stop=False, is_transpose=True)
+                nc.tensor.matmul(bank[:, block], lift[t][:, block], ident[:], start=False, stop=True, is_transpose=True)
             nc.scalar.copy(turned[t][:], bank[:])
 
         def turn_back(t):
-            bank = banks[5 + t]
+            bank = banks[BACK_BANKS[t]]
             for j in range(0, S, P):
                 nc.tensor.transpose(bank[:, j : j + P], turned[t][:, j : j + P], ident[:])
-            for c, (a, b) in enumerate(OUT_CHUNKS):
-                nc.scalar.copy(res[c][:, t, :], bank[:, a:b])
+            nc.scalar.copy(result[:, t, :], bank[:])
+
+        def larger_n5(t, a, b):
+            st_n5 = sb("st_n5_%d_%d" % (t, a), [P, b - a], F32)
+            nc.vector.tensor_copy(st_n5[:], st[t][:].indirect(entries(n5_list, a, b)))
+            nc.vector.tensor_tensor(result[:, t, a:b], st_n5[:], st[t][:, a:b], ALU.max)
 
         scores(0)
-        step(0)
+        less_n4(0)
         scores(1)
-        step(1)
-        differ(0)
+        less_n4(1)
+        excess_n5(0)
         scores(2)
-        differ(1)
-        lifted(0)
+        excess_n5(1)
+        positive_part(0)
         scores(3)
-        step(2)
-        lifted(1)
-        step(3)
-        turn(0)
-        turn(1)
+        less_n4(2, "st_copy1")
+        larger_n5(2, 0, HALF)
+        larger_n5(2, HALF, S)
+        nc.sync.dma_start(out_rows[:, 2, :], result[:, 2, :])
+        positive_part(1)
+        less_n4(3)
+        sum_turned(0)
+        sum_turned(1)
         turn_back(0)
         turn_back(1)
+        nc.scalar.dma_start(out_rows[:, :2, :], result[:, :2, :])
 
-        ow = sb("ow", [P, S], I32)
-        osc = sb("osc", [P, S], U8)
-        out_rows = out_0.rearrange("(p t) j -> p t j", t=PACK)
+        res_words = sb("res_words", [P, S], I32)
+        res_scales = sb("res_scales", [P, S], U8)
         out_words = out_1[0].rearrange("p n r -> p (n r)").bitcast(I32)
         for c, (a, b) in enumerate(OUT_CHUNKS):
-            n = b - a
-            other = sb("other%d" % c, [P, 2, n], F32, tag=("s_win3", "s_plain3")[c % 2])
-            rb = sb("rb%d" % c, [P, PACK * n], BF16)
-            for t in (2, 3):
-                nc.vector.tensor_copy(other[:, t - 2, :], st[t][:].indirect(n5_l[:, a // 16 : b // 16]))
-            for t in (2, 3):
-                nc.vector.tensor_tensor(res[c][:, t, :], other[:, t - 2, :], st[t][:, a:b], ALU.max)
-            nc.sync.dma_start(out_rows[:, :, a:b], res[c][:])
+            rounded = sb("rounded%d" % c, [P, PACK * (b - a)], BF16)
+            larger_n5(3, a, b)
             if b < S:
-                nc.scalar.copy(interleaved(rb[:]), planar(res[c][:]))
+                nc.scalar.copy(interleaved(rounded[:]), planar(result[:, :, a:b]))
             else:
-                nc.vector.tensor_copy(interleaved(rb[:]), planar(res[c][:]))
-            nc.vector.quantize_mx(ow[:, a:b].bitcast(FP8X4), osc[:, a:b], rb[:])
-            if c != 1:
-                first = min(a, HALF)
-                nc.sync.dma_start(out_words[:, first:b], ow[:, first:b])
-        for q in range(4):
+                nc.vector.tensor_copy(interleaved(rounded[:]), planar(result[:, :, a:b]))
+            nc.vector.quantize_mx(res_words[:, a:b].bitcast(FP8X4), res_scales[:, a:b], rounded[:])
+            if b % HALF == 0:
+                done = slice(b - HALF, b)
+                nc.sync.dma_start(out_rows[:, 3, done], result[:, 3, done])
+                nc.sync.dma_start(out_words[:, done], res_words[:, done])
+        for q in range(QUADRANTS):
             queue = nc.sync if q % 2 == 0 else nc.scalar
-            queue.dma_start(out_2[0, 4 * q : 4 * q + 4, :].bitcast(I32), osc[32 * q : 32 * q + 4, :].bitcast(I32))
+            queue.dma_start(
+                out_2[0, 4 * q : 4 * q + 4, :].bitcast(I32), res_scales[32 * q : 32 * q + 4, :].bitcast(I32)
+            )

from contextlib import ExitStack

import concourse.mybir as mybir
from concourse.masks import make_identity

FLOPS = 2 * 512 * 512 * 512 * 2

F32 = mybir.dt.float32
BF16 = mybir.dt.bfloat16
I32 = mybir.dt.int32
U32 = mybir.dt.uint32
U16 = mybir.dt.uint16
U8 = mybir.dt.uint8
FP8X4 = mybir.dt.float8_e4m3fn_x4
ACT = mybir.ActivationFunctionType
ALU = mybir.AluOpType

P = 128
PACK = 4
QUADRANTS = 4
PER_COLUMN = 16
T = 2048
S = 512
HALF = S // 2
SCORE_SCALE = 0.0625

Y_TILE_ON_VECTOR = 1
Z_CHUNKS = ((0, 64), (64, 128), (128, 256), (256, 384), (384, 512))
SCORE_PARTS = (
    ((0, 256, 4), (256, 384, 5), (384, 512, 6)),
    ((0, 256, 1), (256, 512, 7)),
    ((0, 512, 2),),
    ((0, 512, 3),),
)
SUM_TILES = (0, 1)
SUM_BANKS = (0, 4)
BACK_BANKS = (5, 6)
OUT_CHUNKS = ((0, 256), (256, 384), (384, 512))


def tile_picked_candoddshopmx_none_po_kernel(
    tc, x_words, x_scales, w1_words, w1_scales, gs, offs, n1, n2, n3, cand, n4, n5, out_0, out_1, out_2
):
    nc = tc.nc
    with ExitStack() as ctx:
        held = ctx.enter_context(tc.tile_pool(name="held", bufs=1))
        psum = ctx.enter_context(tc.psum_pool(name="psum", bufs=1))

        def sb(name, shape, dtype, after=None):
            return held.tile(shape, dtype, name=name, tag=after or name, align_bytes=64)

        def load_list(name, src):
            tile = sb(name, [P, S // PER_COLUMN], U16)
            nc.sync.dma_start(tile[:], src)
            return tile

        def load_scales(name, src, width, queues):
            tile = sb(name, [P, width], U8)
            nc.vector.memset(tile[:].bitcast(I32), 0)
            for q in range(QUADRANTS):
                queues[q].dma_start(
                    tile[32 * q : 32 * q + 4, :].bitcast(I32), src[0, 4 * q : 4 * q + 4, :].bitcast(I32)
                )
            return tile

        def load_words(name, src, width, queue):
            tile = sb(name, [P, width], I32)
            queue.dma_start(tile[:], src[0].rearrange("p n r -> p (n r)").bitcast(I32))
            return tile

        def deal(name, src, dtype, engine, first, count, after=None):
            tile = sb(name, [P, count * P], dtype, after)
            run = 4 if dtype == I32 else P
            engine.tensor_copy(
                tile[:].rearrange("p (t c i) -> p c t i", t=count, i=run),
                src[:].rearrange("p (c i t) -> p c t i", t=PACK, i=run)[:, :, first : first + count, :],
            )
            return tile

        def wide_window(name):
            tile = sb(name, [P, 2 * S], F32)
            nc.vector.memset(tile[:, S:], 0.0)
            return tile

        def product(out, words, scales, block, rhs_words, rhs_scales):
            nc.tensor.matmul_mx(
                out,
                lhsT=words[:, P * block : P * (block + 1)].bitcast(FP8X4),
                lhsT_scale=scales[:, P * block : P * (block + 1)],
                rhs=rhs_words.bitcast(FP8X4),
                rhs_scale=rhs_scales,
                start=True,
                stop=True,
            )

        def interleaved(ap):
            return ap.rearrange("p (c i t) -> p c t i", i=2, t=PACK)

        def planar(ap):
            return ap.rearrange("p t (c i) -> p c t i", i=2)

        def half(h):
            return slice(h * HALF, (h + 1) * HALF)

        def entries(list_tile, a, b):
            return list_tile[:, a // PER_COLUMN : b // PER_COLUMN]

        def half_entries(list_tile, h):
            return entries(list_tile, h * HALF, (h + 1) * HALF)

        offs_list = load_list("offs_list", offs)
        w_words = load_words("w_words", w1_words, S, nc.scalar)
        n1_list = load_list("n1_list", n1)
        table_scales = load_scales("table_scales", x_scales, T, (nc.sync, nc.sync, nc.scalar, nc.scalar))
        table_words = load_words("table_words", x_words, T, nc.sync)
        neg_s = [wide_window("neg_s%d" % t) for t in range(PACK)]
        w_scales = load_scales("w_scales", w1_scales, S, (nc.scalar,) * QUADRANTS)
        n2_list = load_list("n2_list", n2)
        n3_list = load_list("n3_list", n3)
        cand_list = load_list("cand_list", cand)
        gain = sb("gain", [P, PACK], F32)
        nc.sync.dma_start(gain[:], gs.rearrange("(p t) o -> p (t o)", t=PACK))
        n4_list = load_list("n4_list", n4)
        n5_list = load_list("n5_list", n5)

        ex = [sb("ex%d" % t, [P, S], F32) for t in range(PACK)]
        half_y = [sb("half_y%d" % t, [P, S], F32) for t in range(PACK)]
        banks = [psum.tile([P, S], F32, name="bank%d" % b) for b in range(8)]

        w_words_dealt = deal("w_words_dealt", w_words, I32, nc.vector, 0, PACK)
        pick_words = sb("pick_words", [P, S], I32)
        pick_scales = sb("pick_scales", [P, S], U8)
        nc.vector.tensor_copy(pick_words[:].bitcast(U32), table_words[:].bitcast(U32).indirect(offs_list[:]))
        nc.vector.tensor_copy(pick_scales[:], table_scales[:].indirect(offs_list[:]))
        w_scales_dealt = deal("w_scales_dealt", w_scales, U8, nc.gpsimd, 0, PACK)
        for t in range(PACK):
            product(banks[t][:], w_words_dealt, w_scales_dealt, t, pick_words[:], pick_scales[:])

        cand_words = sb("cand_words", [P, S], I32)
        cand_scales = sb("cand_scales", [P, S], U8)
        nc.vector.tensor_copy(cand_words[:].bitcast(U32), table_words[:].bitcast(U32).indirect(cand_list[:]))
        nc.vector.tensor_copy(cand_scales[:], table_scales[:].indirect(cand_list[:]))
        cand_words_dealt = [deal("cand_words_dealt0", cand_words, I32, nc.vector, 0, 2)]
        cand_scales_dealt = [deal("cand_scales_dealt0", cand_scales, U8, nc.vector, 0, 2)]

        ex_n2 = [sb("ex_n2_%d" % t, [P, S], F32) for t in range(PACK)]
        num = [sb("num%d" % h, [P, PACK, HALF], F32) for h in range(2)]
        den = [sb("den%d" % h, [P, PACK, HALF], F32) for h in range(2)]
        ex_copy_last = sb("ex_copy_last", [P, S], F32)
        for t in range(PACK):
            ex_copy = [den[h][:, t + 1, :] if t + 1 < PACK else ex_copy_last[:, half(h)] for h in range(2)]
            nc.scalar.activation(ex[t][:], banks[t][:], ACT.Exp, scale=0.5)
            for h in range(2):
                nc.sync.dma_start(ex_copy[h], ex[t][:, half(h)])
            if t == Y_TILE_ON_VECTOR:
                nc.vector.tensor_scalar(half_y[t][:], banks[t][:], 0.5, None, ALU.mult)
            else:
                nc.scalar.activation(half_y[t][:], banks[t][:], ACT.Copy, scale=0.5)
            for h in range(2):
                nc.scalar.activation(ex_n2[t][:, half(h)], half_y[t][:].indirect(half_entries(n2_list, h)), ACT.Exp)
            for h in range(2):
                nc.vector.tensor_tensor(
                    den[h][:, t, :], ex[t][:].indirect(half_entries(n3_list, h)), ex_n2[t][:, half(h)], ALU.add
                )
                nc.vector.tensor_tensor(
                    num[h][:, t, :], ex[t][:].indirect(half_entries(n1_list, h)), ex_copy[h], ALU.add
                )

        z_words = sb("z_words", [P, S], I32)
        z_scales = sb("z_scales", [P, S], U8)
        for c, (a, b) in enumerate(Z_CHUNKS):
            n = b - a
            inside = slice(a % HALF, a % HALF + n)
            ln_num = sb("ln_num%d" % c, [P, PACK * n], F32)
            ln_den = sb("ln_den%d" % c, [P, PACK * n], F32)
            odds = sb("odds%d" % c, [P, n, PACK], F32)
            z = sb("z%d" % c, [P, n, PACK], BF16)
            nc.scalar.activation(interleaved(ln_num[:]), planar(num[a // HALF][:, :, inside]), ACT.Ln)
            nc.scalar.activation(interleaved(ln_den[:]), planar(den[a // HALF][:, :, inside]), ACT.Ln)
            nc.vector.tensor_tensor(odds[:].rearrange("p n t -> p (n t)"), ln_num[:], ln_den[:], ALU.subtract)
            nc.vector.tensor_tensor(z[:], odds[:], gain[:].unsqueeze(1).to_broadcast([P, n, PACK]), ALU.mult)
            nc.vector.quantize_mx(
                z_words[:, a:b].bitcast(FP8X4), z_scales[:, a:b], z[:].rearrange("p n t -> p (n t)")
            )

        last = len(Z_CHUNKS) - 1
        cand_scales_dealt.append(deal("cand_scales_dealt1", cand_scales, U8, nc.vector, 2, 2, "odds%d" % last))
        cand_words_dealt.append(deal("cand_words_dealt1", cand_words, I32, nc.vector, 2, 2, "z%d" % last))

        s = [sb("s%d" % t, [P, S], F32) for t in range(PACK)]
        st = {}
        result = sb("result", [P, PACK, S], F32)
        out_rows = out_0.rearrange("(p t) j -> p t j", t=PACK)
        st_copy = [sb("st_copy%d" % t, [P, S], F32) for t in SUM_TILES]
        excess = [sb("excess%d" % t, [P, S], F32) for t in SUM_TILES]
        lift = [sb("lift%d" % t, [P, S], F32) for t in SUM_TILES]
        turned = [sb("turned%d" % t, [P, S], F32) for t in SUM_TILES]
        ident = sb("ident", [P, P], F32)
        make_identity(nc, ident[:])

        def scores(t):
            for a, b, which in SCORE_PARTS[t]:
                bank = banks[which]
                product(
                    bank[:, a:b],
                    cand_words_dealt[t // 2],
                    cand_scales_dealt[t // 2],
                    t % 2,
                    z_words[:, a:b],
                    z_scales[:, a:b],
                )
                nc.scalar.activation(neg_s[t][:, a:b], bank[:, a:b], ACT.Copy, scale=-SCORE_SCALE)
                nc.scalar.activation(s[t][:, a:b], bank[:, a:b], ACT.Copy, scale=SCORE_SCALE)

        def less_n4(t, after=None):
            st[t] = sb("st%d" % t, [P, S], F32, after)
            nc.vector.tensor_tensor(st[t][:], neg_s[t][:].indirect(n4_list[:]), s[t][:], ALU.add)

        def excess_n5(t):
            nc.scalar.copy(st_copy[t][:], st[t][:])
            for h in range(2):
                nc.vector.tensor_tensor(
                    excess[t][:, half(h)],
                    st[t][:].indirect(half_entries(n5_list, h)),
                    st_copy[t][:, half(h)],
                    ALU.subtract,
                )

        def positive_part(t):
            nc.scalar.activation(lift[t][:], excess[t][:], ACT.Relu)

        def sum_turned(t):
            bank = banks[SUM_BANKS[t]]
            for j in range(0, S, P):
                block = slice(j, j + P)
                nc.tensor.matmul(bank[:, block], st[t][:, block], ident[:], start=True, stop=False, is_transpose=True)
                nc.tensor.matmul(bank[:, block], lift[t][:, block], ident[:], start=False, stop=True, is_transpose=True)
            nc.scalar.copy(turned[t][:], bank[:])

        def turn_back(t):
            bank = banks[BACK_BANKS[t]]
            for j in range(0, S, P):
                nc.tensor.transpose(bank[:, j : j + P], turned[t][:, j : j + P], ident[:])
            nc.scalar.copy(result[:, t, :], bank[:])

        def larger_n5(t, a, b):
            st_n5 = sb("st_n5_%d_%d" % (t, a), [P, b - a], F32)
            nc.vector.tensor_copy(st_n5[:], st[t][:].indirect(entries(n5_list, a, b)))
            nc.vector.tensor_tensor(result[:, t, a:b], st_n5[:], st[t][:, a:b], ALU.max)

        scores(0)
        less_n4(0)
        scores(1)
        less_n4(1)
        excess_n5(0)
        scores(2)
        excess_n5(1)
        positive_part(0)
        scores(3)
        less_n4(2, "st_copy1")
        larger_n5(2, 0, HALF)
        larger_n5(2, HALF, S)
        nc.sync.dma_start(out_rows[:, 2, :], result[:, 2, :])
        positive_part(1)
        less_n4(3)
        sum_turned(0)
        sum_turned(1)
        turn_back(0)
        turn_back(1)
        nc.scalar.dma_start(out_rows[:, :2, :], result[:, :2, :])

        res_words = sb("res_words", [P, S], I32)
        res_scales = sb("res_scales", [P, S], U8)
        out_words = out_1[0].rearrange("p n r -> p (n r)").bitcast(I32)
        for c, (a, b) in enumerate(OUT_CHUNKS):
            rounded = sb("rounded%d" % c, [P, PACK * (b - a)], BF16)
            larger_n5(3, a, b)
            if b < S:
                nc.scalar.copy(interleaved(rounded[:]), planar(result[:, :, a:b]))
            else:
                nc.vector.tensor_copy(interleaved(rounded[:]), planar(result[:, :, a:b]))
            nc.vector.quantize_mx(res_words[:, a:b].bitcast(FP8X4), res_scales[:, a:b], rounded[:])
            if b % HALF == 0:
                done = slice(b - HALF, b)
                nc.sync.dma_start(out_rows[:, 3, done], result[:, 3, done])
                nc.sync.dma_start(out_words[:, done], res_words[:, done])
        for q in range(QUADRANTS):
            queue = nc.sync if q % 2 == 0 else nc.scalar
            queue.dma_start(
                out_2[0, 4 * q : 4 * q + 4, :].bitcast(I32), res_scales[32 * q : 32 * q + 4, :].bitcast(I32)
            )
